import numpy as np
import ml_dtypes


def mxq(x, axis, fmt="e4m3"):
    dtype, down = {"e4m3": (ml_dtypes.float8_e4m3fn, 7), "e5m2": (ml_dtypes.float8_e5m2, 14)}[fmt]
    v = np.moveaxis(np.asarray(x, np.float32).astype(ml_dtypes.bfloat16).astype(np.float64), axis, -1)
    blocks = v.reshape(v.shape[:-1] + (-1, 32))
    amax = np.abs(blocks).max(-1, keepdims=True)
    byte = np.maximum(np.where(amax > 0, np.frexp(amax)[1] - 1 + 127, 0) - down, 1)
    scale = np.exp2(byte - 127.0)
    codes = (blocks / scale).astype(np.float32).astype(dtype).astype(np.float64)
    return np.moveaxis((codes * scale).reshape(v.shape), -1, axis)


WIDE = False


def mx_kscale(k):
    if not WIDE:
        return np.ones(k)
    levels = np.array([10, -10, 5, -5, 0])
    if k % 512:
        return np.exp2(np.random.permutation(np.resize(levels, k // 32))).repeat(32)
    a = np.empty((k // 512, 16))
    for p in range(k // 512):
        a[p, :8] = np.random.permutation(np.resize(levels, 8))
        for g in range(8):
            far = levels[np.abs(levels - a[p, g]) >= 10]
            a[p, g + 8] = far[np.random.randint(len(far))]
    return np.exp2(a.ravel()).repeat(32)


def f64(x):
    return np.asarray(x).astype(np.float64)


def striped8(idx):
    return np.asarray(idx).reshape(8, -1, 16).transpose(0, 2, 1).reshape(128, -1).astype(np.uint16)


def unstriped8(offs):
    return offs.reshape(8, 16, -1).transpose(0, 2, 1).reshape(8, -1).astype(np.int64)


def pick8(x, idx, run):
    r = np.arange(len(x))
    return x[r[:, None], idx[r % (8 * run) // run]]


E2M1 = np.array([0.0, 0.5, 1.0, 1.5, 2.0, 3.0, 4.0, 6.0, -0.0, -0.5, -1.0, -1.5, -2.0, -3.0, -4.0, -6.0])


def pack_weight(w, fmt):
    k, n = w.shape
    w = f64(np.asarray(w, np.float32).astype(ml_dtypes.bfloat16)).reshape(k // 32, 32, n)
    amax = np.abs(w).max(1)
    if fmt == "e4m3":
        byte = np.frexp(amax)[1] - 1 + 127 - 7
    else:
        mant, ex = np.frexp(amax / 6.0)
        byte = np.where(mant > 0.5, ex, ex - 1) + 127
    byte = np.clip(np.where(amax > 0, byte, 1), 1, 254)
    scaled = (w * np.exp2(127.0 - byte)[:, None, :]).reshape(k, n).astype(np.float32)
    by_word = np.ascontiguousarray(scaled.reshape(k // 512, 128, 4, n).transpose(0, 1, 3, 2))
    if fmt == "e4m3":
        words = by_word.astype(ml_dtypes.float8_e4m3fn).view(np.uint8)
    else:
        c = by_word.astype(ml_dtypes.float4_e2m1fn).view(np.uint8) & 0xF
        words = (c[..., 0::2] | (c[..., 1::2] << 4)).reshape(k // 512, 128, 2 * n)
    return np.ascontiguousarray(words), np.ascontiguousarray(byte.astype(np.uint8).reshape(k // 512, 16, n))


def unpack_weight(words, scales, fmt):
    g, _, n = scales.shape
    words = np.ascontiguousarray(words).reshape(g, 128, n, -1)
    if fmt == "e4m3":
        vals = words.view(ml_dtypes.float8_e4m3fn).astype(np.float64)
    else:
        nib = np.empty((g, 128, n, 4), np.uint8)
        nib[..., 0::2] = words & 0xF
        nib[..., 1::2] = words >> 4
        vals = E2M1[nib]
    vals = vals * np.repeat(np.exp2(scales.astype(np.float64) - 127.0), 8, axis=1)[..., None]
    return vals.transpose(0, 1, 3, 2).reshape(g * 512, n)


D, T, I, Q, G = 512, 1024, 512, 128, 64


def setup_inputs():
    n = np.random.standard_normal
    idx = np.stack([np.random.permutation(T)[:I] for _ in range(8)])
    idx2 = np.stack([np.random.permutation(T)[:I] for _ in range(8)])
    idx3 = np.stack([np.random.permutation(T)[:I] for _ in range(8)])
    fd = mx_kscale(D)
    keysp = pack_weight(n((D, T)) / fd[:, None], "e4m3")
    return {
        "query": (n((D, Q)) * 0.9 / np.sqrt(D) * fd[:, None]).astype(np.float32),
        "keys_words": keysp[0],
        "keys_scales": keysp[1],
        "lam": (np.random.uniform(0.7, 1.3, (Q, 1))).astype(np.float32),
        "old": (np.random.uniform(0.0, 2.0, (Q, T))).astype(np.float32),
        "fade": (np.random.uniform(0.3, 0.9, (Q, 1))).astype(np.float32),
        "offs": striped8(idx),
        "offs2": striped8(idx2),
        "offs3": striped8(idx3),
    }


def reference(query, keys_words, keys_scales, lam, old, fade, offs, offs2, offs3):
    idx = unstriped8(offs)
    idx2 = unstriped8(offs2)
    idx3 = unstriped8(offs3)
    keysu = unpack_weight(keys_words, keys_scales, "e4m3")
    queryq = mxq(f64(query), 0, "e4m3")
    a = queryq.T @ keysu
    s = pick8(a, idx, 16) * f64(lam) - np.abs(pick8(a, idx2, 16) - pick8(a, idx3, 16))
    p = np.exp(s)
    pg = p.reshape(Q, G, I // G).sum(axis=2)
    z0 = np.sum(pg, axis=1, keepdims=True)
    k0 = 1.0 / (z0 - pg)
    kr = np.repeat(k0, I // G, axis=1)
    w = p * kr
    ws = w * 64.0
    wf = np.zeros((Q, T))
    wf[np.arange(Q)[:, None], idx[np.arange(Q) % 128 // 16]] = ws
    y = f64(old) * f64(fade) + wf
    return y

@@ -1,0 +1,159 @@
+from contextlib import ExitStack
+
+import concourse.mybir as mybir
+
+D, T, I, Q, G = 512, 1024, 512, 128, 64
+RUN = I // G
+
+FLOPS = 2 * D * Q * T
+
+F32 = mybir.dt.float32
+BF16 = mybir.dt.bfloat16
+U32 = mybir.dt.uint32
+I32 = mybir.dt.int32
+U16 = mybir.dt.uint16
+U8 = mybir.dt.uint8
+FP8X4 = mybir.dt.float8_e4m3fn_x4
+ALU = mybir.AluOpType
+ACT = mybir.ActivationFunctionType
+AXIS = mybir.AxisListType
+
+P = 128
+PACK = 4
+PLANES = 4
+PLANE_COLS = T // PLANES
+PER_COL = 16
+
+
+def tile_attend_betweentwo_outside_counts_heads_kernel(
+    tc, query, keys_words, keys_scales, lam, old, fade, offs, offs2, offs3, out
+):
+    nc = tc.nc
+    with ExitStack() as ctx:
+        pool = ctx.enter_context(tc.tile_pool(name="held", bufs=1))
+        psum = ctx.enter_context(tc.psum_pool(name="psum", bufs=1))
+
+        list1 = pool.tile([P, I // PER_COL], U16, name="list1")
+        list2 = pool.tile([P, I // PER_COL], U16, name="list2")
+        list3 = pool.tile([P, I // PER_COL], U16, name="list3")
+        q_raw = pool.tile([P, PACK, Q], F32, name="q_raw")
+        key_planes = pool.tile([P, PLANE_COLS], U8, name="key_planes", align_bytes=64)
+        key_words = [pool.tile([P, T // 2], U32, name=f"key_words{h}", align_bytes=64) for h in range(2)]
+        lam_sb = pool.tile([P, 1], F32, name="lam_sb")
+        fade_sb = pool.tile([P, 1], F32, name="fade_sb")
+        old_sb = pool.tile([P, T], F32, name="old_sb")
+        placed = pool.tile([P, T], F32, name="placed")
+
+        nc.vector.memset(key_planes[:].bitcast(I32), 0)
+        nc.sync.dma_start(out=q_raw[:], in_=query.rearrange("(p j) q -> p j q", j=PACK))
+        scale_words = keys_scales[0].bitcast(I32)
+        for quad in range(4):
+            nc.scalar.dma_start(
+                out=key_planes[32 * quad : 32 * quad + 16, :].bitcast(I32),
+                in_=scale_words[4 * quad : 4 * quad + 4, :].rearrange("r (j c) -> j r c", j=PLANES),
+            )
+        words = keys_words[0].rearrange("p n t -> p (n t)").bitcast(I32)
+        for h in range(2):
+            nc.sync.dma_start(out=key_words[h][:].bitcast(I32), in_=words[:, h * (T // 2) : (h + 1) * (T // 2)])
+        nc.sync.dma_start(list3[:], offs3)
+        nc.sync.dma_start(list1[:], offs)
+        nc.sync.dma_start(list2[:], offs2)
+        nc.gpsimd.dma_start(out=lam_sb[:], in_=lam)
+        nc.gpsimd.dma_start(out=fade_sb[:], in_=fade)
+        nc.sync.dma_start(out=old_sb[:], in_=old)
+        nc.gpsimd.memset(placed[:], 0.0)
+
+        q_grouped = pool.tile([P, Q, PACK], BF16, name="q_grouped", align_bytes=64)
+        nc.vector.tensor_copy(out=q_grouped[:], in_=q_raw[:].rearrange("p j q -> p q j"))
+        q_words = pool.tile([P, Q], U32, name="q_words", align_bytes=64)
+        q_plane = pool.tile([P, Q], U8, name="q_plane", align_bytes=64)
+        nc.vector.quantize_mx(
+            out=q_words[:].bitcast(FP8X4), scales=q_plane[:], in_=q_grouped[:].rearrange("p q j -> p (q j)")
+        )
+
+        a = pool.tile([P, T], F32, name="a")
+        widths = [256, 256, 256, 128, 128]
+        start = 0
+        for n, width in enumerate(widths):
+            plane, col = divmod(start, PLANE_COLS)
+            half, word = divmod(start, T // 2)
+            bank = psum.tile([P, width], F32, name=f"bank{n}")
+            nc.tensor.matmul_mx(
+                out=bank[:],
+                lhsT=q_words[:].bitcast(FP8X4),
+                lhsT_scale=q_plane[:],
+                rhs=key_words[half][:, word : word + width].bitcast(FP8X4),
+                rhs_scale=key_planes[4 * plane : P, col : col + width],
+                start=True,
+                stop=True,
+            )
+            if n % 2 == 0:
+                nc.scalar.copy(out=a[:, start : start + width], in_=bank[:])
+            else:
+                nc.vector.tensor_copy(out=a[:, start : start + width], in_=bank[:])
+            start = start + width
+
+        H = I // 2
+        first = pool.tile([P, I], F32, name="first")
+        third = pool.tile([P, I], F32, name="third")
+        diff = pool.tile([P, I], F32, name="diff")
+        gap = pool.tile([P, I], F32, name="gap")
+        s = pool.tile([P, I], F32, name="s")
+        p = pool.tile([P, I], F32, name="p")
+        pg = pool.tile([P, G], F32, name="pg")
+        z = [pool.tile([P, 1], F32, name=f"z{h}") for h in range(2)]
+        sl = [slice(0, H), slice(H, I)]
+        cl = [slice(0, H // PER_COL), slice(H // PER_COL, I // PER_COL)]
+        gl = [slice(0, G // 2), slice(G // 2, G)]
+
+        nc.scalar.activation(third[:, sl[0]], a[:].indirect(list3[:, cl[0]]), ACT.Copy)
+        nc.vector.tensor_copy(first[:, sl[0]], a[:].indirect(list1[:, cl[0]]))
+        nc.scalar.activation(third[:, sl[1]], a[:].indirect(list3[:, cl[1]]), ACT.Copy)
+        nc.vector.tensor_tensor(diff[:, sl[0]], a[:].indirect(list2[:, cl[0]]), third[:, sl[0]], ALU.subtract)
+        nc.scalar.activation(gap[:, sl[0]], diff[:, sl[0]], ACT.Abs)
+        nc.vector.tensor_tensor(diff[:, sl[1]], a[:].indirect(list2[:, cl[1]]), third[:, sl[1]], ALU.subtract)
+        nc.scalar.activation(first[:, sl[1]], a[:].indirect(list1[:, cl[1]]), ACT.Copy)
+        nc.vector.scalar_tensor_tensor(
+            s[:, sl[0]], first[:, sl[0]], lam_sb[:], gap[:, sl[0]], ALU.mult, ALU.subtract
+        )
+        nc.vector.scalar_tensor_tensor(gap[:, sl[1]], diff[:, sl[1]], -1.0, diff[:, sl[1]], ALU.mult, ALU.max)
+        nc.scalar.activation(p[:, sl[0]], s[:, sl[0]], ACT.Exp, accum_out=z[0][:])
+        nc.vector.scalar_tensor_tensor(
+            s[:, sl[1]], first[:, sl[1]], lam_sb[:], gap[:, sl[1]], ALU.mult, ALU.subtract
+        )
+        nc.vector.tensor_reduce(pg[:, gl[0]], p[:, sl[0]].rearrange("q (g r) -> q g r", r=RUN), AXIS.X, ALU.add)
+        nc.scalar.activation(p[:, sl[1]], s[:, sl[1]], ACT.Exp, accum_out=z[1][:])
+        nc.vector.tensor_reduce(pg[:, gl[1]], p[:, sl[1]].rearrange("q (g r) -> q g r", r=RUN), AXIS.X, ALU.add)
+
+        neg_rest = pool.tile([P, G], F32, name="neg_rest")
+        neg_k0 = pool.tile([P, G], F32, name="neg_k0")
+        kr = pool.tile([P, I], F32, name="kr")
+        nc.vector.tensor_scalar(neg_rest[:], pg[:], z[0][:], z[1][:], ALU.subtract, ALU.subtract)
+        cuts = [(0, 16), (16, G)]
+        for g0, g1 in cuts:
+            nc.vector.reciprocal(neg_k0[:, g0:g1], neg_rest[:, g0:g1])
+            nc.scalar.activation(
+                kr[:, g0 * RUN : g1 * RUN].rearrange("q (g r) -> q g r", r=RUN),
+                neg_k0[:, g0:g1].unsqueeze(2).to_broadcast([P, g1 - g0, RUN]),
+                ACT.Copy,
+                scale=-64.0,
+            )
+        for g0, g1 in cuts:
+            slots = slice(g0 * RUN, g1 * RUN)
+            nc.vector.tensor_tensor(
+                placed[:].indirect(list1[:, g0 * RUN // PER_COL : g1 * RUN // PER_COL]),
+                p[:, slots],
+                kr[:, slots],
+                ALU.mult,
+            )
+
+        result = pool.tile([P, T], F32, name="result")
+        start = 0
+        for n, width in enumerate([320, 320, 256, 128]):
+            cols = slice(start, start + width)
+            nc.vector.scalar_tensor_tensor(
+                result[:, cols], old_sb[:, cols], fade_sb[:], placed[:, cols], ALU.mult, ALU.add
+            )
+            queue = nc.sync if n % 2 == 0 else nc.scalar
+            queue.dma_start(out=out[:, cols], in_=result[:, cols])
+            start = start + width

@@ -44,27 +44,29 @@ def tile_attend_betweentwo_outside_counts_heads_kernel(
         old_sb = pool.tile([P, T], F32, name="old_sb")
         placed = pool.tile([P, T], F32, name="placed")
 
-        nc.vector.memset(key_planes[:].bitcast(I32), 0)
-        nc.sync.dma_start(out=q_raw[:], in_=query.rearrange("(p j) q -> p j q", j=PACK))
         scale_words = keys_scales[0].bitcast(I32)
+        words = keys_words[0].rearrange("p n t -> p (n t)").bitcast(I32)
+        nc.sync.dma_start(out=q_raw[:], in_=query.rearrange("(p j) q -> p j q", j=PACK))
         for quad in range(4):
-            nc.scalar.dma_start(
+            queue = nc.scalar if quad < 2 else nc.sync
+            queue.dma_start(
                 out=key_planes[32 * quad : 32 * quad + 16, :].bitcast(I32),
                 in_=scale_words[4 * quad : 4 * quad + 4, :].rearrange("r (j c) -> j r c", j=PLANES),
             )
-        words = keys_words[0].rearrange("p n t -> p (n t)").bitcast(I32)
         for h in range(2):
             nc.sync.dma_start(out=key_words[h][:].bitcast(I32), in_=words[:, h * (T // 2) : (h + 1) * (T // 2)])
         nc.sync.dma_start(list3[:], offs3)
         nc.sync.dma_start(list1[:], offs)
         nc.sync.dma_start(list2[:], offs2)
-        nc.gpsimd.dma_start(out=lam_sb[:], in_=lam)
-        nc.gpsimd.dma_start(out=fade_sb[:], in_=fade)
+        nc.sync.dma_start(out=lam_sb[:], in_=lam)
         nc.sync.dma_start(out=old_sb[:], in_=old)
-        nc.gpsimd.memset(placed[:], 0.0)
+        nc.sync.dma_start(out=fade_sb[:], in_=fade)
+        nc.vector.memset(placed[:], 0.0)
 
         q_grouped = pool.tile([P, Q, PACK], BF16, name="q_grouped", align_bytes=64)
-        nc.vector.tensor_copy(out=q_grouped[:], in_=q_raw[:].rearrange("p j q -> p q j"))
+        q_turned = q_raw[:].rearrange("p j q -> p q j")
+        nc.vector.tensor_copy(out=q_grouped[:, :80, :], in_=q_turned[:, :80, :])
+        nc.scalar.copy(out=q_grouped[:, 80:, :], in_=q_turned[:, 80:, :])
         q_words = pool.tile([P, Q], U32, name="q_words", align_bytes=64)
         q_plane = pool.tile([P, Q], U8, name="q_plane", align_bytes=64)
         nc.vector.quantize_mx(
@@ -109,35 +111,42 @@ def tile_attend_betweentwo_outside_counts_heads_kernel(
         nc.scalar.activation(third[:, sl[0]], a[:].indirect(list3[:, cl[0]]), ACT.Copy)
         nc.vector.tensor_copy(first[:, sl[0]], a[:].indirect(list1[:, cl[0]]))
         nc.scalar.activation(third[:, sl[1]], a[:].indirect(list3[:, cl[1]]), ACT.Copy)
-        nc.vector.tensor_tensor(diff[:, sl[0]], a[:].indirect(list2[:, cl[0]]), third[:, sl[0]], ALU.subtract)
-        nc.scalar.activation(gap[:, sl[0]], diff[:, sl[0]], ACT.Abs)
-        nc.vector.tensor_tensor(diff[:, sl[1]], a[:].indirect(list2[:, cl[1]]), third[:, sl[1]], ALU.subtract)
         nc.scalar.activation(first[:, sl[1]], a[:].indirect(list1[:, cl[1]]), ACT.Copy)
-        nc.vector.scalar_tensor_tensor(
-            s[:, sl[0]], first[:, sl[0]], lam_sb[:], gap[:, sl[0]], ALU.mult, ALU.subtract
-        )
-        nc.vector.scalar_tensor_tensor(gap[:, sl[1]], diff[:, sl[1]], -1.0, diff[:, sl[1]], ALU.mult, ALU.max)
-        nc.scalar.activation(p[:, sl[0]], s[:, sl[0]], ACT.Exp, accum_out=z[0][:])
-        nc.vector.scalar_tensor_tensor(
-            s[:, sl[1]], first[:, sl[1]], lam_sb[:], gap[:, sl[1]], ALU.mult, ALU.subtract
-        )
-        nc.vector.tensor_reduce(pg[:, gl[0]], p[:, sl[0]].rearrange("q (g r) -> q g r", r=RUN), AXIS.X, ALU.add)
-        nc.scalar.activation(p[:, sl[1]], s[:, sl[1]], ACT.Exp, accum_out=z[1][:])
-        nc.vector.tensor_reduce(pg[:, gl[1]], p[:, sl[1]].rearrange("q (g r) -> q g r", r=RUN), AXIS.X, ALU.add)
+        for h in range(2):
+            nc.vector.tensor_tensor(diff[:, sl[h]], a[:].indirect(list2[:, cl[h]]), third[:, sl[h]], ALU.subtract)
+        for n in range(4):
+            q4 = slice(n * (I // 4), (n + 1) * (I // 4))
+            nc.scalar.activation(gap[:, q4], diff[:, q4], ACT.Abs)
+            nc.vector.scalar_tensor_tensor(s[:, q4], first[:, q4], lam_sb[:], gap[:, q4], ALU.mult, ALU.subtract)
+        for h in range(2):
+            nc.scalar.activation(p[:, sl[h]], s[:, sl[h]], ACT.Exp, accum_out=z[h][:])
 
         neg_rest = pool.tile([P, G], F32, name="neg_rest")
         neg_k0 = pool.tile([P, G], F32, name="neg_k0")
         kr = pool.tile([P, I], F32, name="kr")
-        nc.vector.tensor_scalar(neg_rest[:], pg[:], z[0][:], z[1][:], ALU.subtract, ALU.subtract)
-        cuts = [(0, 16), (16, G)]
-        for g0, g1 in cuts:
+
+        def invert(g0, g1):
             nc.vector.reciprocal(neg_k0[:, g0:g1], neg_rest[:, g0:g1])
+
+        def spread(g0, g1):
             nc.scalar.activation(
                 kr[:, g0 * RUN : g1 * RUN].rearrange("q (g r) -> q g r", r=RUN),
                 neg_k0[:, g0:g1].unsqueeze(2).to_broadcast([P, g1 - g0, RUN]),
                 ACT.Copy,
                 scale=-64.0,
             )
+
+        nc.vector.tensor_reduce(pg[:, gl[0]], p[:, sl[0]].rearrange("q (g r) -> q g r", r=RUN), AXIS.X, ALU.add)
+        nc.vector.tensor_scalar(neg_rest[:, gl[0]], pg[:, gl[0]], z[0][:], z[1][:], ALU.subtract, ALU.subtract)
+        nc.vector.tensor_reduce(pg[:, gl[1]], p[:, sl[1]].rearrange("q (g r) -> q g r", r=RUN), AXIS.X, ALU.add)
+        invert(0, 16)
+        spread(0, 16)
+        invert(16, 32)
+        spread(16, 32)
+        nc.vector.tensor_scalar(neg_rest[:, gl[1]], pg[:, gl[1]], z[0][:], z[1][:], ALU.subtract, ALU.subtract)
+        invert(32, G)
+        spread(32, G)
+        cuts = [(0, 16), (16, G)]
         for g0, g1 in cuts:
             slots = slice(g0 * RUN, g1 * RUN)
             nc.vector.tensor_tensor(
@@ -149,7 +158,7 @@ def tile_attend_betweentwo_outside_counts_heads_kernel(
 
         result = pool.tile([P, T], F32, name="result")
         start = 0
-        for n, width in enumerate([320, 320, 256, 128]):
+        for n, width in enumerate([128, 256, 256, 256, 128]):
             cols = slice(start, start + width)
             nc.vector.scalar_tensor_tensor(
                 result[:, cols], old_sb[:, cols], fade_sb[:], placed[:, cols], ALU.mult, ALU.add

from contextlib import ExitStack

import concourse.mybir as mybir

D, T, I, Q, G = 512, 1024, 512, 128, 64
RUN = I // G

FLOPS = 2 * D * Q * T

F32 = mybir.dt.float32
BF16 = mybir.dt.bfloat16
U32 = mybir.dt.uint32
I32 = mybir.dt.int32
U16 = mybir.dt.uint16
U8 = mybir.dt.uint8
FP8X4 = mybir.dt.float8_e4m3fn_x4
ALU = mybir.AluOpType
ACT = mybir.ActivationFunctionType
AXIS = mybir.AxisListType

P = 128
PACK = 4
PLANES = 4
PLANE_COLS = T // PLANES
PER_COL = 16


def tile_attend_betweentwo_outside_counts_heads_kernel(
    tc, query, keys_words, keys_scales, lam, old, fade, offs, offs2, offs3, out
):
    nc = tc.nc
    with ExitStack() as ctx:
        pool = ctx.enter_context(tc.tile_pool(name="held", bufs=1))
        psum = ctx.enter_context(tc.psum_pool(name="psum", bufs=1))

        list1 = pool.tile([P, I // PER_COL], U16, name="list1")
        list2 = pool.tile([P, I // PER_COL], U16, name="list2")
        list3 = pool.tile([P, I // PER_COL], U16, name="list3")
        q_raw = pool.tile([P, PACK, Q], F32, name="q_raw")
        key_planes = pool.tile([P, PLANE_COLS], U8, name="key_planes", align_bytes=64)
        key_words = [pool.tile([P, T // 2], U32, name=f"key_words{h}", align_bytes=64) for h in range(2)]
        lam_sb = pool.tile([P, 1], F32, name="lam_sb")
        fade_sb = pool.tile([P, 1], F32, name="fade_sb")
        old_sb = pool.tile([P, T], F32, name="old_sb")
        placed = pool.tile([P, T], F32, name="placed")

        scale_words = keys_scales[0].bitcast(I32)
        words = keys_words[0].rearrange("p n t -> p (n t)").bitcast(I32)
        nc.sync.dma_start(out=q_raw[:], in_=query.rearrange("(p j) q -> p j q", j=PACK))
        for quad in range(4):
            queue = nc.scalar if quad < 2 else nc.sync
            queue.dma_start(
                out=key_planes[32 * quad : 32 * quad + 16, :].bitcast(I32),
                in_=scale_words[4 * quad : 4 * quad + 4, :].rearrange("r (j c) -> j r c", j=PLANES),
            )
        for h in range(2):
            nc.sync.dma_start(out=key_words[h][:].bitcast(I32), in_=words[:, h * (T // 2) : (h + 1) * (T // 2)])
        nc.sync.dma_start(list3[:], offs3)
        nc.sync.dma_start(list1[:], offs)
        nc.sync.dma_start(list2[:], offs2)
        nc.sync.dma_start(out=lam_sb[:], in_=lam)
        nc.sync.dma_start(out=old_sb[:], in_=old)
        nc.sync.dma_start(out=fade_sb[:], in_=fade)
        nc.vector.memset(placed[:], 0.0)

        q_grouped = pool.tile([P, Q, PACK], BF16, name="q_grouped", align_bytes=64)
        q_turned = q_raw[:].rearrange("p j q -> p q j")
        nc.vector.tensor_copy(out=q_grouped[:, :80, :], in_=q_turned[:, :80, :])
        nc.scalar.copy(out=q_grouped[:, 80:, :], in_=q_turned[:, 80:, :])
        q_words = pool.tile([P, Q], U32, name="q_words", align_bytes=64)
        q_plane = pool.tile([P, Q], U8, name="q_plane", align_bytes=64)
        nc.vector.quantize_mx(
            out=q_words[:].bitcast(FP8X4), scales=q_plane[:], in_=q_grouped[:].rearrange("p q j -> p (q j)")
        )

        a = pool.tile([P, T], F32, name="a")
        widths = [256, 256, 256, 128, 128]
        start = 0
        for n, width in enumerate(widths):
            plane, col = divmod(start, PLANE_COLS)
            half, word = divmod(start, T // 2)
            bank = psum.tile([P, width], F32, name=f"bank{n}")
            nc.tensor.matmul_mx(
                out=bank[:],
                lhsT=q_words[:].bitcast(FP8X4),
                lhsT_scale=q_plane[:],
                rhs=key_words[half][:, word : word + width].bitcast(FP8X4),
                rhs_scale=key_planes[4 * plane : P, col : col + width],
                start=True,
                stop=True,
            )
            if n % 2 == 0:
                nc.scalar.copy(out=a[:, start : start + width], in_=bank[:])
            else:
                nc.vector.tensor_copy(out=a[:, start : start + width], in_=bank[:])
            start = start + width

        H = I // 2
        first = pool.tile([P, I], F32, name="first")
        third = pool.tile([P, I], F32, name="third")
        diff = pool.tile([P, I], F32, name="diff")
        gap = pool.tile([P, I], F32, name="gap")
        s = pool.tile([P, I], F32, name="s")
        p = pool.tile([P, I], F32, name="p")
        pg = pool.tile([P, G], F32, name="pg")
        z = [pool.tile([P, 1], F32, name=f"z{h}") for h in range(2)]
        sl = [slice(0, H), slice(H, I)]
        cl = [slice(0, H // PER_COL), slice(H // PER_COL, I // PER_COL)]
        gl = [slice(0, G // 2), slice(G // 2, G)]

        nc.scalar.activation(third[:, sl[0]], a[:].indirect(list3[:, cl[0]]), ACT.Copy)
        nc.vector.tensor_copy(first[:, sl[0]], a[:].indirect(list1[:, cl[0]]))
        nc.scalar.activation(third[:, sl[1]], a[:].indirect(list3[:, cl[1]]), ACT.Copy)
        nc.scalar.activation(first[:, sl[1]], a[:].indirect(list1[:, cl[1]]), ACT.Copy)
        for h in range(2):
            nc.vector.tensor_tensor(diff[:, sl[h]], a[:].indirect(list2[:, cl[h]]), third[:, sl[h]], ALU.subtract)
        for n in range(4):
            q4 = slice(n * (I // 4), (n + 1) * (I // 4))
            nc.scalar.activation(gap[:, q4], diff[:, q4], ACT.Abs)
            nc.vector.scalar_tensor_tensor(s[:, q4], first[:, q4], lam_sb[:], gap[:, q4], ALU.mult, ALU.subtract)
        for h in range(2):
            nc.scalar.activation(p[:, sl[h]], s[:, sl[h]], ACT.Exp, accum_out=z[h][:])

        neg_rest = pool.tile([P, G], F32, name="neg_rest")
        neg_k0 = pool.tile([P, G], F32, name="neg_k0")
        kr = pool.tile([P, I], F32, name="kr")

        def invert(g0, g1):
            nc.vector.reciprocal(neg_k0[:, g0:g1], neg_rest[:, g0:g1])

        def spread(g0, g1):
            nc.scalar.activation(
                kr[:, g0 * RUN : g1 * RUN].rearrange("q (g r) -> q g r", r=RUN),
                neg_k0[:, g0:g1].unsqueeze(2).to_broadcast([P, g1 - g0, RUN]),
                ACT.Copy,
                scale=-64.0,
            )

        nc.vector.tensor_reduce(pg[:, gl[0]], p[:, sl[0]].rearrange("q (g r) -> q g r", r=RUN), AXIS.X, ALU.add)
        nc.vector.tensor_scalar(neg_rest[:, gl[0]], pg[:, gl[0]], z[0][:], z[1][:], ALU.subtract, ALU.subtract)
        nc.vector.tensor_reduce(pg[:, gl[1]], p[:, sl[1]].rearrange("q (g r) -> q g r", r=RUN), AXIS.X, ALU.add)
        invert(0, 16)
        spread(0, 16)
        invert(16, 32)
        spread(16, 32)
        nc.vector.tensor_scalar(neg_rest[:, gl[1]], pg[:, gl[1]], z[0][:], z[1][:], ALU.subtract, ALU.subtract)
        invert(32, G)
        spread(32, G)
        cuts = [(0, 16), (16, G)]
        for g0, g1 in cuts:
            slots = slice(g0 * RUN, g1 * RUN)
            nc.vector.tensor_tensor(
                placed[:].indirect(list1[:, g0 * RUN // PER_COL : g1 * RUN // PER_COL]),
                p[:, slots],
                kr[:, slots],
                ALU.mult,
            )

        result = pool.tile([P, T], F32, name="result")
        start = 0
        for n, width in enumerate([128, 256, 256, 256, 128]):
            cols = slice(start, start + width)
            nc.vector.scalar_tensor_tensor(
                result[:, cols], old_sb[:, cols], fade_sb[:], placed[:, cols], ALU.mult, ALU.add
            )
            queue = nc.sync if n % 2 == 0 else nc.scalar
            queue.dma_start(out=out[:, cols], in_=result[:, cols])
            start = start + width
